import numpy as np
import ml_dtypes

BF16 = ml_dtypes.bfloat16


def bf(x):
    return np.asarray(x, np.float32).astype(BF16)


def f32(x):
    return np.asarray(x, np.float32)


def f64(x):
    return np.asarray(x).astype(np.float64)


def striped(idx):
    return np.tile(idx.reshape(-1, 16).T, (8, 1))


def rows(idx, k):
    return np.tile(idx, (k, 1))


def look(tab, idx):
    return np.take_along_axis(f64(tab), rows(idx, len(tab)), axis=1)


K, S, D, V, N = 256, 256, 3, 64, 192


def setup_inputs():
    return {"tab": f32(np.random.standard_normal((K, S))), "ctr": f32(np.random.standard_normal((K, V))), "offs": striped(np.random.permutation(S)[:N])}


def reference(tab, ctr, offs):
    idx = offs[:16].T.reshape(-1)
    x = sum(np.maximum(look(tab, idx[d * V:(d + 1) * V]) - f64(ctr), 0.0) for d in range(D))
    return x

@@ -1,0 +1,36 @@
+import concourse.mybir as mybir
+
+P = 128
+GROUP = 16
+F32, U16 = mybir.dt.float32, mybir.dt.uint16
+ALU = mybir.AluOpType
+
+
+def tile_lookup_edge_sub_out_kernel(tc, tab, ctr, offs, out):
+    nc = tc.nc
+    rows, width = tab.shape
+    nodes = ctr.shape[1]
+    neighbours = offs.shape[1] * GROUP // nodes
+    piece = nodes // GROUP
+
+    with tc.tile_pool(name="held", bufs=1) as held:
+        offsets = held.tile([P, offs.shape[1]], U16, name="offsets")
+        nc.sync.dma_start(offsets[:], offs)
+        for b in range(rows // P):
+            block = slice(b * P, (b + 1) * P)
+            window = held.tile([P, width], F32, name=f"window{b}")
+            centre = held.tile([P, nodes], F32, name=f"centre{b}")
+            nc.sync.dma_start(window[:], tab[block, :])
+            nc.sync.dma_start(centre[:], ctr[block, :])
+            total = None
+            for d in range(neighbours):
+                diff = held.tile([P, nodes], F32, name=f"diff{b}_{d}")
+                nc.vector.tensor_tensor(
+                    diff[:], window[:].indirect(offsets[:, d * piece:(d + 1) * piece]), centre[:], ALU.subtract)
+                summed = held.tile([P, nodes], F32, name=f"sum{b}_{d}")
+                if total is None:
+                    nc.vector.tensor_scalar_max(summed[:], diff[:], 0.0)
+                else:
+                    nc.vector.scalar_tensor_tensor(summed[:], diff[:], 0.0, total[:], ALU.max, ALU.add)
+                total = summed
+            nc.sync.dma_start(out[block, :], total[:])

@@ -10,27 +10,36 @@ def tile_lookup_edge_sub_out_kernel(tc, tab, ctr, offs, out):
     nc = tc.nc
     rows, width = tab.shape
     nodes = ctr.shape[1]
-    neighbours = offs.shape[1] * GROUP // nodes
+    blocks = rows // P
     piece = nodes // GROUP
+    tab_b = tab.rearrange("(p b) s -> b p s", b=blocks)
 
     with tc.tile_pool(name="held", bufs=1) as held:
         offsets = held.tile([P, offs.shape[1]], U16, name="offsets")
+        centre = held.tile([P, blocks, nodes], F32, name="centre")
+        windows = [held.tile([P, width], F32, name=f"window{b}") for b in range(blocks)]
+        diffs = [held.tile([P, blocks, nodes], F32, name=f"diff{d}") for d in range(3)]
+        sum1 = held.tile([P, blocks, nodes], F32, name="sum1")
+        sum2 = held.tile([P, blocks, nodes], F32, name="sum2")
+        sum3 = held.tile([P, blocks, nodes], F32, name="sum3")
+
         nc.sync.dma_start(offsets[:], offs)
-        for b in range(rows // P):
-            block = slice(b * P, (b + 1) * P)
-            window = held.tile([P, width], F32, name=f"window{b}")
-            centre = held.tile([P, nodes], F32, name=f"centre{b}")
-            nc.sync.dma_start(window[:], tab[block, :])
-            nc.sync.dma_start(centre[:], ctr[block, :])
-            total = None
-            for d in range(neighbours):
-                diff = held.tile([P, nodes], F32, name=f"diff{b}_{d}")
-                nc.vector.tensor_tensor(
-                    diff[:], window[:].indirect(offsets[:, d * piece:(d + 1) * piece]), centre[:], ALU.subtract)
-                summed = held.tile([P, nodes], F32, name=f"sum{b}_{d}")
-                if total is None:
-                    nc.vector.tensor_scalar_max(summed[:], diff[:], 0.0)
-                else:
-                    nc.vector.scalar_tensor_tensor(summed[:], diff[:], 0.0, total[:], ALU.max, ALU.add)
-                total = summed
-            nc.sync.dma_start(out[block, :], total[:])
+        nc.scalar.dma_start(windows[0][:], tab_b[0])
+        nc.sync.dma_start(centre[:], ctr.rearrange("(p b) v -> p b v", b=blocks))
+        nc.sync.dma_start(windows[1][:], tab_b[1])
+
+        def difference(d, b):
+            nc.vector.tensor_tensor(
+                diffs[d][:, b, :], windows[b][:].indirect(offsets[:, d * piece:(d + 1) * piece]),
+                centre[:, b, :], ALU.subtract)
+
+        for b in range(blocks):
+            difference(0, b)
+            difference(1, b)
+        nc.vector.tensor_scalar_max(sum1[:], diffs[0][:], 0.0)
+        difference(2, 0)
+        nc.vector.scalar_tensor_tensor(sum2[:], diffs[1][:], 0.0, sum1[:], ALU.max, ALU.add)
+        difference(2, 1)
+        for b in range(blocks):
+            nc.vector.scalar_tensor_tensor(sum3[:, b, :], diffs[2][:, b, :], 0.0, sum2[:, b, :], ALU.max, ALU.add)
+        nc.sync.dma_start(out.rearrange("(p b) v -> p b v", b=blocks), sum3[:])

@@ -24,7 +24,7 @@ def tile_lookup_edge_sub_out_kernel(tc, tab, ctr, offs, out):
         sum3 = held.tile([P, blocks, nodes], F32, name="sum3")
 
         nc.sync.dma_start(offsets[:], offs)
-        nc.scalar.dma_start(windows[0][:], tab_b[0])
+        nc.sync.dma_start(windows[0][:], tab_b[0])
         nc.sync.dma_start(centre[:], ctr.rearrange("(p b) v -> p b v", b=blocks))
         nc.sync.dma_start(windows[1][:], tab_b[1])
 

@@ -2,8 +2,10 @@ import concourse.mybir as mybir
 
 P = 128
 GROUP = 16
+NEIGHBOURS = 3
 F32, U16 = mybir.dt.float32, mybir.dt.uint16
 ALU = mybir.AluOpType
+RELU = mybir.ActivationFunctionType.Relu
 
 
 def tile_lookup_edge_sub_out_kernel(tc, tab, ctr, offs, out):
@@ -12,34 +14,35 @@ def tile_lookup_edge_sub_out_kernel(tc, tab, ctr, offs, out):
     nodes = ctr.shape[1]
     blocks = rows // P
     piece = nodes // GROUP
-    tab_b = tab.rearrange("(p b) s -> b p s", b=blocks)
+    tab_blocks = tab.rearrange("(p b) s -> b p s", b=blocks)
 
     with tc.tile_pool(name="held", bufs=1) as held:
         offsets = held.tile([P, offs.shape[1]], U16, name="offsets")
         centre = held.tile([P, blocks, nodes], F32, name="centre")
         windows = [held.tile([P, width], F32, name=f"window{b}") for b in range(blocks)]
-        diffs = [held.tile([P, blocks, nodes], F32, name=f"diff{d}") for d in range(3)]
-        sum1 = held.tile([P, blocks, nodes], F32, name="sum1")
-        sum2 = held.tile([P, blocks, nodes], F32, name="sum2")
-        sum3 = held.tile([P, blocks, nodes], F32, name="sum3")
+        diffs = [held.tile([P, blocks, nodes], F32, name=f"diff{d}") for d in range(NEIGHBOURS)]
+        sums = [held.tile([P, blocks, nodes], F32, name=f"sum{d}") for d in range(NEIGHBOURS)]
 
         nc.sync.dma_start(offsets[:], offs)
-        nc.sync.dma_start(windows[0][:], tab_b[0])
+        nc.sync.dma_start(windows[0][:], tab_blocks[0])
         nc.sync.dma_start(centre[:], ctr.rearrange("(p b) v -> p b v", b=blocks))
-        nc.sync.dma_start(windows[1][:], tab_b[1])
+        nc.sync.dma_start(windows[1][:], tab_blocks[1])
 
         def difference(d, b):
-            nc.vector.tensor_tensor(
-                diffs[d][:, b, :], windows[b][:].indirect(offsets[:, d * piece:(d + 1) * piece]),
-                centre[:, b, :], ALU.subtract)
+            picked = windows[b][:].indirect(offsets[:, d * piece:(d + 1) * piece])
+            nc.vector.tensor_tensor(diffs[d][:, b, :], picked, centre[:, b, :], ALU.subtract)
+
+        def add_positive_part(d, b):
+            nc.vector.scalar_tensor_tensor(
+                sums[d][:, b, :], diffs[d][:, b, :], 0.0, sums[d - 1][:, b, :], ALU.max, ALU.add)
 
         for b in range(blocks):
             difference(0, b)
+            nc.scalar.activation(sums[0][:, b, :], diffs[0][:, b, :], RELU)
             difference(1, b)
-        nc.vector.tensor_scalar_max(sum1[:], diffs[0][:], 0.0)
-        difference(2, 0)
-        nc.vector.scalar_tensor_tensor(sum2[:], diffs[1][:], 0.0, sum1[:], ALU.max, ALU.add)
-        difference(2, 1)
         for b in range(blocks):
-            nc.vector.scalar_tensor_tensor(sum3[:, b, :], diffs[2][:, b, :], 0.0, sum2[:, b, :], ALU.max, ALU.add)
-        nc.sync.dma_start(out.rearrange("(p b) v -> p b v", b=blocks), sum3[:])
+            add_positive_part(1, b)
+            difference(2, b)
+        for b in range(blocks):
+            add_positive_part(2, b)
+        nc.sync.dma_start(out.rearrange("(p b) v -> p b v", b=blocks), sums[NEIGHBOURS - 1][:])

import concourse.mybir as mybir

P = 128
GROUP = 16
NEIGHBOURS = 3
F32, U16 = mybir.dt.float32, mybir.dt.uint16
ALU = mybir.AluOpType
RELU = mybir.ActivationFunctionType.Relu


def tile_lookup_edge_sub_out_kernel(tc, tab, ctr, offs, out):
    nc = tc.nc
    rows, width = tab.shape
    nodes = ctr.shape[1]
    blocks = rows // P
    piece = nodes // GROUP
    tab_blocks = tab.rearrange("(p b) s -> b p s", b=blocks)

    with tc.tile_pool(name="held", bufs=1) as held:
        offsets = held.tile([P, offs.shape[1]], U16, name="offsets")
        centre = held.tile([P, blocks, nodes], F32, name="centre")
        windows = [held.tile([P, width], F32, name=f"window{b}") for b in range(blocks)]
        diffs = [held.tile([P, blocks, nodes], F32, name=f"diff{d}") for d in range(NEIGHBOURS)]
        sums = [held.tile([P, blocks, nodes], F32, name=f"sum{d}") for d in range(NEIGHBOURS)]

        nc.sync.dma_start(offsets[:], offs)
        nc.sync.dma_start(windows[0][:], tab_blocks[0])
        nc.sync.dma_start(centre[:], ctr.rearrange("(p b) v -> p b v", b=blocks))
        nc.sync.dma_start(windows[1][:], tab_blocks[1])

        def difference(d, b):
            picked = windows[b][:].indirect(offsets[:, d * piece:(d + 1) * piece])
            nc.vector.tensor_tensor(diffs[d][:, b, :], picked, centre[:, b, :], ALU.subtract)

        def add_positive_part(d, b):
            nc.vector.scalar_tensor_tensor(
                sums[d][:, b, :], diffs[d][:, b, :], 0.0, sums[d - 1][:, b, :], ALU.max, ALU.add)

        for b in range(blocks):
            difference(0, b)
            nc.scalar.activation(sums[0][:, b, :], diffs[0][:, b, :], RELU)
            difference(1, b)
        for b in range(blocks):
            add_positive_part(1, b)
            difference(2, b)
        for b in range(blocks):
            add_positive_part(2, b)
        nc.sync.dma_start(out.rearrange("(p b) v -> p b v", b=blocks), sums[NEIGHBOURS - 1][:])
